import numpy as np
import ml_dtypes


def mxq(x, axis, fmt="e4m3"):
    dtype, down = {"e4m3": (ml_dtypes.float8_e4m3fn, 7), "e5m2": (ml_dtypes.float8_e5m2, 14)}[fmt]
    v = np.moveaxis(np.asarray(x, np.float32).astype(ml_dtypes.bfloat16).astype(np.float64), axis, -1)
    blocks = v.reshape(v.shape[:-1] + (-1, 32))
    amax = np.abs(blocks).max(-1, keepdims=True)
    byte = np.maximum(np.where(amax > 0, np.frexp(amax)[1] - 1 + 127, 0) - down, 1)
    scale = np.exp2(byte - 127.0)
    codes = (blocks / scale).astype(np.float32).astype(dtype).astype(np.float64)
    return np.moveaxis((codes * scale).reshape(v.shape), -1, axis)


WIDE = False


def mx_kscale(k):
    if not WIDE:
        return np.ones(k)
    levels = np.array([10, -10, 5, -5, 0])
    if k % 512:
        return np.exp2(np.random.permutation(np.resize(levels, k // 32))).repeat(32)
    a = np.empty((k // 512, 16))
    for p in range(k // 512):
        a[p, :8] = np.random.permutation(np.resize(levels, 8))
        for g in range(8):
            far = levels[np.abs(levels - a[p, g]) >= 10]
            a[p, g + 8] = far[np.random.randint(len(far))]
    return np.exp2(a.ravel()).repeat(32)


def f64(x):
    return np.asarray(x).astype(np.float64)


def striped(idx):
    return np.tile(idx.reshape(-1, 16).T, (8, 1)).astype(np.uint16)


def unstriped(offs):
    return offs[:16].T.reshape(-1).astype(np.int64)


def striped8(idx):
    return np.concatenate([x.reshape(-1, 16).T for x in idx]).astype(np.uint16)


def runs(offs, k):
    lists = np.stack([offs[16 * r : 16 * r + 16].T.reshape(-1) for r in range(8)]).astype(np.int64)
    return lists[np.arange(k) % 512 // 64]


def pack_weight(w):
    k, n = w.shape
    w = f64(np.asarray(w, np.float32).astype(ml_dtypes.bfloat16)).reshape(k // 32, 32, n)
    amax = np.abs(w).max(1)
    byte = np.clip(np.where(amax > 0, np.frexp(amax)[1] - 1 + 127 - 7, 1), 1, 254)
    scaled = (w * np.exp2(127.0 - byte)[:, None, :]).reshape(k, n).astype(np.float32)
    words = np.ascontiguousarray(scaled.reshape(k // 512, 128, 4, n).transpose(0, 1, 3, 2)).astype(ml_dtypes.float8_e4m3fn).view(np.uint8)
    return words, np.ascontiguousarray(byte.astype(np.uint8).reshape(k // 512, 16, n))


def unpack_weight(words, scales):
    g, p, n, _ = words.shape
    vals = np.ascontiguousarray(words).view(ml_dtypes.float8_e4m3fn).astype(np.float64) * np.repeat(np.exp2(scales.astype(np.float64) - 127.0), 8, axis=1)[..., None]
    return vals.transpose(0, 1, 3, 2).reshape(g * 512, n)


E2M1 = np.array([0.0, 0.5, 1.0, 1.5, 2.0, 3.0, 4.0, 6.0, -0.0, -0.5, -1.0, -1.5, -2.0, -3.0, -4.0, -6.0])


def pack_fp4(w):
    k, n = w.shape
    w = f64(np.asarray(w, np.float32).astype(ml_dtypes.bfloat16)).reshape(k // 32, 32, n)
    amax = np.abs(w).max(1)
    mant, ex = np.frexp(amax / 6.0)
    byte = np.clip(np.where(amax > 0, np.where(mant > 0.5, ex, ex - 1) + 127, 1), 1, 254)
    scaled = (w * np.exp2(127.0 - byte)[:, None, :]).reshape(k, n).astype(np.float32)
    c = np.ascontiguousarray(scaled.reshape(k // 512, 128, 4, n).transpose(0, 1, 3, 2)).astype(ml_dtypes.float4_e2m1fn).view(np.uint8) & 0xF
    words = (c[..., 0::2] | (c[..., 1::2] << 4)).reshape(k // 512, 128, 2 * n)
    return np.ascontiguousarray(words), np.ascontiguousarray(byte.astype(np.uint8).reshape(k // 512, 16, n))


def unpack_fp4(words, scales):
    g, _, n = scales.shape
    words = np.ascontiguousarray(words).reshape(g, 128, n, 2)
    nib = np.empty((g, 128, n, 4), np.uint8)
    nib[..., 0::2] = words & 0xF
    nib[..., 1::2] = words >> 4
    vals = E2M1[nib] * np.repeat(np.exp2(scales.astype(np.float64) - 127.0), 8, axis=1)[..., None]
    return vals.transpose(0, 1, 3, 2).reshape(g * 512, n)


def sigmoid(v):
    return 1.0 / (1.0 + np.exp(-np.maximum(v, -700.0)))

def planes(y):
    n, m = y.shape
    v = y.astype(np.float32).astype(ml_dtypes.bfloat16).astype(np.float64).reshape(n // 32, 32, m)
    top = np.abs(v).max(1)
    byte = np.clip(np.where(top > 0, np.frexp(top)[1] - 1 + 127 - 7, 1), 1, 254)
    codes = (v * np.exp2(127.0 - byte)[:, None, :]).reshape(n, m).astype(np.float32).astype(ml_dtypes.float8_e4m3fn).view(np.uint8)
    words = codes.reshape(n // 512, 128, 4, m).transpose(0, 1, 3, 2)
    return np.ascontiguousarray(words), np.ascontiguousarray(byte.astype(np.uint8).reshape(n // 512, 16, m))


K, T, S, V, H, W = 512, 2048, 512, 512, 512, 256


def setup_inputs():
    n = np.random.standard_normal
    s = mx_kscale(K)[:, None]
    u = mx_kscale(S)
    packed_xT = pack_weight(n((K, T)) * s)
    packed_w1 = pack_fp4(n((K, H)) / np.sqrt(K) / s)
    packed_w2 = pack_fp4(n((K, H)) / np.sqrt(K) / s)
    packed_w3 = pack_fp4(n((K, H)) / np.sqrt(K) / s)
    perm = np.stack([np.random.permutation(V) for _ in range(8)])
    return {
        "x_words": packed_xT[0],
        "x_scales": packed_xT[1],
        "w1_words": packed_w1[0],
        "w1_scales": packed_w1[1],
        "w2_words": packed_w2[0],
        "w2_scales": packed_w2[1],
        "w3_words": packed_w3[0],
        "w3_scales": packed_w3[1],
        "ga": (np.random.uniform(0.5, 1.5, (H, 1)) * u[:, None]).astype(np.float32),
        "gb": (np.random.uniform(0.5, 1.5, (H, 1)) / u[:, None]).astype(np.float32),
        "offs": striped(np.random.permutation(T)[:S]),
        "two": striped(np.random.permutation(T)[:S]),
        "n1": striped8(np.stack([np.random.permutation(S) for _ in range(8)])),
        "n2": striped8(np.stack([np.random.permutation(S) for _ in range(8)])),
        "three": striped(np.random.permutation(T)[:V]),
        "n3": striped8(perm[:, :W]),
        "n4": striped8(perm[:, W:]),
        "n5": striped8(np.stack([np.random.permutation(V) for _ in range(8)])),
        "n6": striped8(np.stack([np.random.permutation(V) for _ in range(8)])),
        "n7": striped8(np.stack([np.random.permutation(V) for _ in range(8)])),
    }


def reference(x_words, x_scales, w1_words, w1_scales, w2_words, w2_scales, w3_words, w3_scales, ga, gb, offs, two, n1, n2, three, n3, n4, n5, n6, n7):
    xq = unpack_weight(x_words, x_scales)[:, unstriped(offs)]
    y = unpack_fp4(w1_words, w1_scales).T @ xq
    x_two = unpack_weight(x_words, x_scales)[:, unstriped(two)]
    d = unpack_fp4(w2_words, w2_scales).T @ x_two
    z = f64(ga) * (y[np.arange(H)[:, None], runs(n1, H)] - (np.tanh(d) * (d[np.arange(H)[:, None], runs(n2, H)])))
    x_three = unpack_weight(x_words, x_scales)[:, unstriped(three)]
    b = unpack_fp4(w3_words, w3_scales).T @ x_three
    pb = b[np.arange(H)[:, None], runs(n4, H)]
    pa = b[np.arange(H)[:, None], runs(n3, H)]
    rb = pb * sigmoid(pb - pa)
    ra = pa * sigmoid(pa - pb)
    ds = np.zeros((H, V))
    ds[np.arange(H)[:, None], runs(n3, H)] = ra
    dt = ds.copy()
    dt[np.arange(H)[:, None], runs(n4, H)] = rb
    z2 = f64(gb) * dt
    s = 0.0625 * ((mxq(z, 0, "e4m3").T @ mxq(z2, 0, "e4m3")))
    out_0 = s + s[np.arange(S)[:, None], runs(n5, S)] - (np.maximum(s[np.arange(S)[:, None], runs(n6, S)], s[np.arange(S)[:, None], runs(n7, S)]))
    return (out_0,) + planes(out_0)

@@ -1,0 +1,232 @@
+from contextlib import ExitStack
+
+import concourse.mybir as mybir
+from concourse.masks import make_identity
+
+K, T, S, W = 512, 2048, 512, 256
+FLOPS = 4 * 2 * 512 * 512 * 512
+
+F32 = mybir.dt.float32
+BF16 = mybir.dt.bfloat16
+I32 = mybir.dt.int32
+U32 = mybir.dt.uint32
+U16 = mybir.dt.uint16
+U8 = mybir.dt.uint8
+FP8X4 = mybir.dt.float8_e4m3fn_x4
+FP4X4 = mybir.dt.float4_e2m1fn_x4
+ALU = mybir.AluOpType
+ACT = mybir.ActivationFunctionType
+
+P = 128
+PACK = 4
+HALF = 256
+
+
+def tile_picked_twksoftbdueltrim_none_po_kernel(
+    tc, x_words, x_scales, w1_words, w1_scales, w2_words, w2_scales, w3_words, w3_scales,
+    ga, gb, offs, two, n1, n2, three, n3, n4, n5, n6, n7, out_0, out_1, out_2,
+):
+    nc = tc.nc
+    with ExitStack() as ctx:
+        keep = ctx.enter_context(tc.tile_pool(name="keep", bufs=1))
+        psum = ctx.enter_context(tc.psum_pool(name="psum", bufs=8))
+
+        def load_list(name, src):
+            t = keep.tile(list(src.shape), U16, name=name)
+            nc.sync.dma_start(t[:], src)
+            return t
+
+        def load_scale_rows(tile, src, eng):
+            eng.memset(tile[:].bitcast(I32), 0)
+            for q in range(4):
+                nc.sync.dma_start(tile[32 * q : 32 * q + 4, :].bitcast(I32), src[0, 4 * q : 4 * q + 4, :].bitcast(I32))
+
+        def load_weight(name, words, scales):
+            raw_w = keep.tile([P, 2 * S], U8, name=name + "_raw_words")
+            raw_s = keep.tile([P, S], U8, name=name + "_raw_scales")
+            nc.sync.dma_start(raw_w[:].bitcast(I32), words[0].bitcast(I32))
+            load_scale_rows(raw_s, scales, nc.gpsimd)
+            return raw_w, raw_s
+
+        def deal_weight(name, raw):
+            dealt_w = keep.tile([P, 2 * S], U8, name=name + "_words", align_bytes=64)
+            dealt_s = keep.tile([P, S], U8, name=name + "_scales", align_bytes=64)
+            for dst, src in ((dealt_w, raw[0]), (dealt_s, raw[1])):
+                nc.gpsimd.tensor_copy(
+                    dst[:].bitcast(I32).rearrange("p (t b r) -> p t b r", t=PACK, b=16),
+                    src[:].bitcast(I32).rearrange("p (b t r) -> p t b r", t=PACK, b=16),
+                )
+            return dealt_w, dealt_s
+
+        def pick(name, dtype, table, lst):
+            t = keep.tile([P, S], dtype, name=name, align_bytes=64)
+            nc.vector.tensor_copy(t[:], table[:].indirect(lst[:]))
+            return t
+
+        def project(weight, words, scales, t):
+            acc = psum.tile([P, S], F32, name="acc")
+            nc.tensor.matmul_mx(
+                acc[:],
+                lhsT=weight[0][:, 2 * P * t : 2 * P * (t + 1)].bitcast(FP4X4),
+                lhsT_scale=weight[1][:, P * t : P * (t + 1)],
+                rhs=words[:].bitcast(FP8X4),
+                rhs_scale=scales[:],
+                start=True,
+                stop=True,
+            )
+            return acc
+
+        xs = keep.tile([P, T], U8, name="xs")
+        xw = keep.tile([P, T], U32, name="xw")
+        load_scale_rows(xs, x_scales, nc.vector)
+        l_three = load_list("three", three)
+        l_two = load_list("two", two)
+        l_offs = load_list("offs", offs)
+        nc.sync.dma_start(xw[:].bitcast(I32), x_words[0].rearrange("p n t -> p (n t)").bitcast(I32))
+        raw3 = load_weight("w3", w3_words, w3_scales)
+        l3 = load_list("n3", n3)
+        l4 = load_list("n4", n4)
+        gain_rows = keep.tile([P, P], F32, name="gain_rows")
+        ident = keep.tile([P, P], F32, name="ident")
+        nc.gpsimd.memset(gain_rows[:], 0.0)
+        make_identity(nc, ident[:])
+        for i, g in enumerate((ga, gb)):
+            nc.sync.dma_start(
+                gain_rows[PACK * i : PACK * (i + 1), :].rearrange("t (b r) -> t b r", r=8),
+                g.rearrange("(b t r) o -> t b (r o)", t=PACK, r=8),
+            )
+        raw2 = load_weight("w2", w2_words, w2_scales)
+        raw1 = load_weight("w1", w1_words, w1_scales)
+        l2 = load_list("n2", n2)
+        l1 = load_list("n1", n1)
+        l6 = load_list("n6", n6)
+        l7 = load_list("n7", n7)
+        l5 = load_list("n5", n5)
+
+        s_three = pick("s_three", U8, xs, l_three)
+        s_two = pick("s_two", U8, xs, l_two)
+        s_offs = pick("s_offs", U8, xs, l_offs)
+        w_three = pick("w_three", U32, xw, l_three)
+        w3 = deal_weight("w3", raw3)
+        w_two = pick("w_two", U32, xw, l_two)
+        w_offs = pick("w_offs", U32, xw, l_offs)
+
+        gain_t = psum.tile([P, S], F32, name="acc")
+        nc.tensor.transpose(gain_t[:, 0:P], gain_rows[:], ident[:])
+        gains = keep.tile([P, 2 * PACK], F32, name="gains")
+        nc.scalar.copy(gains[:], gain_t[:, 0 : 2 * PACK])
+
+        b_win = []
+        for t in range(PACK):
+            acc = project(w3, w_three, s_three, t)
+            win = keep.tile([P, S], F32, name="b%d" % t)
+            nc.scalar.copy(win[:], acc[:])
+            b_win.append(win)
+        w2 = deal_weight("w2", raw2)
+        w1 = deal_weight("w1", raw1)
+        pairs, gates = [], []
+        for t in range(PACK):
+            pair = keep.tile([P, 2, W], F32, name="scratch%d" % t)
+            nc.vector.tensor_copy(pair[:, 0, :], b_win[t][:].indirect(l3[:]))
+            nc.vector.tensor_copy(pair[:, 1, :], b_win[t][:].indirect(l4[:]))
+            pairs.append(pair)
+        for t in range(PACK):
+            diff = keep.tile([P, W], F32, name="diff%d" % t)
+            nc.vector.tensor_tensor(diff[:], pairs[t][:, 0, :], pairs[t][:, 1, :], ALU.subtract)
+            gate = keep.tile([P, 2, W], F32, name="gate%d" % t)
+            nc.scalar.activation(gate[:, 0, :], diff[:], ACT.Sigmoid)
+            nc.scalar.activation(gate[:, 1, :], diff[:], ACT.Sigmoid, scale=-1.0)
+            gates.append(gate)
+
+        d_win, y_win, tanh_d = [], [], []
+        for t in range(PACK):
+            acc = project(w2, w_two, s_two, t)
+            win = keep.tile([P, 2 * S], F32, name="d%d" % t)
+            th = keep.tile([P, S], F32, name="tanh%d" % t)
+            nc.scalar.activation(win[:, 0:S], acc[:], ACT.Copy, scale=gains[:, t : t + 1])
+            nc.scalar.activation(th[:], acc[:], ACT.Tanh)
+            d_win.append(win)
+            tanh_d.append(th)
+            acc = project(w1, w_offs, s_offs, t)
+            win = keep.tile([P, S], F32, name="y%d" % t)
+            nc.scalar.activation(win[:], acc[:], ACT.Copy, scale=gains[:, t : t + 1])
+            y_win.append(win)
+
+        dts = [keep.tile([P, S], F32, name="dt%d" % t) for t in range(PACK)]
+        z2_rows = keep.tile([P, PACK, S], BF16, name="z2_rows")
+        for t in range(PACK):
+            nc.vector.tensor_tensor(dts[t][:].indirect(l3[:]), pairs[t][:, 0, :], gates[t][:, 0, :], ALU.mult)
+            nc.vector.tensor_tensor(dts[t][:].indirect(l4[:]), pairs[t][:, 1, :], gates[t][:, 1, :], ALU.mult)
+            nc.scalar.activation(z2_rows[:, t, :], dts[t][:], ACT.Copy, scale=gains[:, PACK + t : PACK + t + 1])
+        z2_bf = keep.tile([P, S, PACK], BF16, name="z2_bf", align_bytes=64)
+        nc.scalar.copy(z2_bf[:], z2_rows[:].rearrange("p t v -> p v t"))
+        z2_w = keep.tile([P, S], U32, name="z2_w", align_bytes=64)
+        z2_s = keep.tile([P, S], U8, name="z2_s", align_bytes=64)
+
+        prods = [keep.tile([P, 2, W], F32, name="scratch%d" % t) for t in range(PACK)]
+        z_bf = keep.tile([P, PACK, P, PACK], BF16, name="z_bf", align_bytes=64)
+        for t in range(PACK):
+            nc.vector.tensor_tensor(prods[t][:].rearrange("p c w -> p (c w)"), d_win[t][:].indirect(l2[:]), tanh_d[t][:], ALU.mult)
+        for c in range(2):
+            ent = slice(16 * c, 16 * (c + 1))
+            z = keep.tile([P, PACK, HALF], F32, name="z%d" % c)
+            for t in range(PACK):
+                nc.vector.tensor_tensor(z[:, t, :], y_win[t][:].indirect(l1[:, ent]), prods[t][:, c, :], ALU.subtract)
+            dst = z_bf[:, :, 64 * c : 64 * (c + 1), :].rearrange("p u m t -> p m u t")
+            src = z[:].rearrange("p t (m u) -> p m u t", u=PACK)
+            if c == 0:
+                nc.scalar.copy(dst, src)
+            else:
+                nc.vector.quantize_mx(z2_w[:].bitcast(FP8X4), z2_s[:], z2_bf[:].rearrange("p v t -> p (v t)"))
+                nc.vector.tensor_copy(dst, src)
+
+        z_w = keep.tile([P, PACK, P], U32, name="z_w", align_bytes=64)
+        z_s = keep.tile([P, PACK, P], U8, name="z_s", align_bytes=64)
+        s_win, s_plain = [], []
+        for u in range(PACK):
+            nc.vector.quantize_mx(z_w[:, u, :].bitcast(FP8X4), z_s[:, u, :], z_bf[:, u].rearrange("p m t -> p (m t)"))
+            acc = psum.tile([P, S], F32, name="acc")
+            nc.tensor.matmul_mx(
+                acc[:], lhsT=z_w[:, u, :].bitcast(FP8X4), lhsT_scale=z_s[:, u, :],
+                rhs=z2_w[:].bitcast(FP8X4), rhs_scale=z2_s[:], start=True, stop=True,
+            )
+            win = keep.tile([P, 2 * S], F32, name="s%d" % u)
+            plain = keep.tile([P, S], F32, name="sp%d" % u)
+            nc.scalar.activation(win[:, 0:S], acc[:], ACT.Copy, scale=0.0625)
+            nc.scalar.activation(plain[:], acc[:], ACT.Copy, scale=0.0625)
+            s_win.append(win)
+            s_plain.append(plain)
+
+        o_bf = keep.tile([P, S, PACK], BF16, name="o_bf", align_bytes=64)
+        o_w = keep.tile([P, S], U32, name="o_w", align_bytes=64)
+        o_s = keep.tile([P, S], U8, name="o_s", align_bytes=64)
+        out_rows = out_0.rearrange("(p u) v -> p u v", u=PACK)
+        out_words = out_1[0].rearrange("p n t -> p (n t)").bitcast(I32)
+        first = keep.tile([P, PACK, S], F32, name="first")
+        second = keep.tile([P, PACK, S], F32, name="second")
+        larger = keep.tile([P, PACK, S], F32, name="larger")
+        for u in range(PACK + 1):
+            if u < PACK:
+                nc.vector.tensor_tensor(first[:, u, :], s_win[u][:].indirect(l6[:]), s_plain[u][:], ALU.subtract)
+            if u > 0:
+                nc.vector.tensor_tensor(larger[:, u - 1, :], first[:, u - 1, :], second[:, u - 1, :], ALU.max)
+            if u < PACK:
+                nc.vector.tensor_tensor(second[:, u, :], s_win[u][:].indirect(l7[:]), s_plain[u][:], ALU.subtract)
+        for c in range(2):
+            cols = slice(HALF * c, HALF * (c + 1))
+            ent = slice(16 * c, 16 * (c + 1))
+            o = keep.tile([P, PACK, HALF], F32, name="o%d" % c)
+            for u in range(PACK):
+                nc.vector.tensor_tensor(o[:, u, :], s_win[u][:].indirect(l5[:, ent]), larger[:, u, cols], ALU.subtract)
+                if u % 2 == 1:
+                    nc.sync.dma_start(out_rows[:, u - 1 : u + 1, cols], o[:, u - 1 : u + 1, :])
+            src = o[:].rearrange("p u v -> p v u")
+            if c == 0:
+                nc.scalar.copy(o_bf[:, cols, :], src)
+            else:
+                nc.vector.tensor_copy(o_bf[:, cols, :], src)
+            nc.vector.quantize_mx(o_w[:, cols].bitcast(FP8X4), o_s[:, cols], o_bf[:, cols, :].rearrange("p v u -> p (v u)"))
+            nc.sync.dma_start(out_words[:, cols], o_w[:, cols].bitcast(I32))
+        for q in range(4):
+            queue = nc.scalar if q % 2 else nc.sync
+            queue.dma_start(out_2[0, 4 * q : 4 * q + 4, :].bitcast(I32), o_s[32 * q : 32 * q + 4, :].bitcast(I32))

@@ -20,6 +20,7 @@ ACT = mybir.ActivationFunctionType
 P = 128
 PACK = 4
 HALF = 256
+CHUNKS = ((0, 256), (256, 384), (384, 512))
 
 
 def tile_picked_twksoftbdueltrim_none_po_kernel(
@@ -78,11 +79,11 @@ def tile_picked_twksoftbdueltrim_none_po_kernel(
 
         xs = keep.tile([P, T], U8, name="xs")
         xw = keep.tile([P, T], U32, name="xw")
-        load_scale_rows(xs, x_scales, nc.vector)
+        load_scale_rows(xs, x_scales, nc.gpsimd)
         l_three = load_list("three", three)
         l_two = load_list("two", two)
-        l_offs = load_list("offs", offs)
         nc.sync.dma_start(xw[:].bitcast(I32), x_words[0].rearrange("p n t -> p (n t)").bitcast(I32))
+        l_offs = load_list("offs", offs)
         raw3 = load_weight("w3", w3_words, w3_scales)
         l3 = load_list("n3", n3)
         l4 = load_list("n4", n4)
@@ -105,9 +106,9 @@ def tile_picked_twksoftbdueltrim_none_po_kernel(
 
         s_three = pick("s_three", U8, xs, l_three)
         s_two = pick("s_two", U8, xs, l_two)
-        s_offs = pick("s_offs", U8, xs, l_offs)
         w_three = pick("w_three", U32, xw, l_three)
         w3 = deal_weight("w3", raw3)
+        s_offs = pick("s_offs", U8, xs, l_offs)
         w_two = pick("w_two", U32, xw, l_two)
         w_offs = pick("w_offs", U32, xw, l_offs)
 
@@ -124,19 +125,36 @@ def tile_picked_twksoftbdueltrim_none_po_kernel(
             b_win.append(win)
         w2 = deal_weight("w2", raw2)
         w1 = deal_weight("w1", raw1)
-        pairs, gates = [], []
-        for t in range(PACK):
-            pair = keep.tile([P, 2, W], F32, name="scratch%d" % t)
-            nc.vector.tensor_copy(pair[:, 0, :], b_win[t][:].indirect(l3[:]))
-            nc.vector.tensor_copy(pair[:, 1, :], b_win[t][:].indirect(l4[:]))
-            pairs.append(pair)
-        for t in range(PACK):
-            diff = keep.tile([P, W], F32, name="diff%d" % t)
-            nc.vector.tensor_tensor(diff[:], pairs[t][:, 0, :], pairs[t][:, 1, :], ALU.subtract)
-            gate = keep.tile([P, 2, W], F32, name="gate%d" % t)
-            nc.scalar.activation(gate[:, 0, :], diff[:], ACT.Sigmoid)
-            nc.scalar.activation(gate[:, 1, :], diff[:], ACT.Sigmoid, scale=-1.0)
-            gates.append(gate)
+        pairs = [keep.tile([P, 2, 2, W], F32, name="pairs%d" % h) for h in range(2)]
+        gates = [keep.tile([P, 2, 2, W], F32, name="gates%d" % h) for h in range(2)]
+        dts = [keep.tile([P, S], F32, name="dt%d" % t) for t in range(PACK)]
+        z2_rows = keep.tile([P, PACK, S], BF16, name="z2_rows")
+        pair_lists = (l3, l4)
+
+        def fetch(t):
+            for side in range(2):
+                nc.vector.tensor_copy(pairs[t // 2][:, side, t % 2, :], b_win[t][:].indirect(pair_lists[side][:]))
+
+        def duel(h):
+            diff = keep.tile([P, 2, W], F32, name="b%d" % (2 - 2 * h))
+            nc.vector.tensor_tensor(diff[:], pairs[h][:, 0], pairs[h][:, 1], ALU.subtract)
+            nc.scalar.activation(gates[h][:, 0], diff[:], ACT.Sigmoid)
+            nc.scalar.activation(gates[h][:, 1], diff[:], ACT.Sigmoid, scale=-1.0)
+
+        def put(h):
+            for side in range(2):
+                for t in (2 * h, 2 * h + 1):
+                    nc.vector.tensor_tensor(
+                        dts[t][:].indirect(pair_lists[side][:]), pairs[h][:, side, t % 2, :], gates[h][:, side, t % 2, :], ALU.mult
+                    )
+                    if side == 1:
+                        nc.scalar.activation(z2_rows[:, t, :], dts[t][:], ACT.Copy, scale=gains[:, PACK + t : PACK + t + 1])
+
+        for t in range(PACK - 1):
+            fetch(t)
+        duel(0)
+        fetch(PACK - 1)
+        duel(1)
 
         d_win, y_win, tanh_d = [], [], []
         for t in range(PACK):
@@ -152,81 +170,108 @@ def tile_picked_twksoftbdueltrim_none_po_kernel(
             nc.scalar.activation(win[:], acc[:], ACT.Copy, scale=gains[:, t : t + 1])
             y_win.append(win)
 
-        dts = [keep.tile([P, S], F32, name="dt%d" % t) for t in range(PACK)]
-        z2_rows = keep.tile([P, PACK, S], BF16, name="z2_rows")
-        for t in range(PACK):
-            nc.vector.tensor_tensor(dts[t][:].indirect(l3[:]), pairs[t][:, 0, :], gates[t][:, 0, :], ALU.mult)
-            nc.vector.tensor_tensor(dts[t][:].indirect(l4[:]), pairs[t][:, 1, :], gates[t][:, 1, :], ALU.mult)
-            nc.scalar.activation(z2_rows[:, t, :], dts[t][:], ACT.Copy, scale=gains[:, PACK + t : PACK + t + 1])
+        put(0)
+        put(1)
         z2_bf = keep.tile([P, S, PACK], BF16, name="z2_bf", align_bytes=64)
         nc.scalar.copy(z2_bf[:], z2_rows[:].rearrange("p t v -> p v t"))
         z2_w = keep.tile([P, S], U32, name="z2_w", align_bytes=64)
         z2_s = keep.tile([P, S], U8, name="z2_s", align_bytes=64)
-
-        prods = [keep.tile([P, 2, W], F32, name="scratch%d" % t) for t in range(PACK)]
-        z_bf = keep.tile([P, PACK, P, PACK], BF16, name="z_bf", align_bytes=64)
+        prods = keep.tile([P, PACK, S], F32, name="pairs1")
         for t in range(PACK):
-            nc.vector.tensor_tensor(prods[t][:].rearrange("p c w -> p (c w)"), d_win[t][:].indirect(l2[:]), tanh_d[t][:], ALU.mult)
-        for c in range(2):
-            ent = slice(16 * c, 16 * (c + 1))
-            z = keep.tile([P, PACK, HALF], F32, name="z%d" % c)
+            nc.vector.tensor_tensor(prods[:, t, :], d_win[t][:].indirect(l2[:]), tanh_d[t][:], ALU.mult)
+
+        z_bf = keep.tile([P, PACK, P, PACK], BF16, name="z_bf", align_bytes=64)
+
+        def quantise_z2(lo, hi):
+            nc.vector.quantize_mx(z2_w[:, lo:hi].bitcast(FP8X4), z2_s[:, lo:hi], z2_bf[:, lo:hi, :].rearrange("p v t -> p (v t)"))
+
+        z_all = keep.tile([P, PACK * S], F32, name="z2_rows")
+        for lo, hi in CHUNKS:
+            last = hi == S
+            z = z_all[:, PACK * lo : PACK * hi].rearrange("p (t j) -> p t j", t=PACK)
             for t in range(PACK):
-                nc.vector.tensor_tensor(z[:, t, :], y_win[t][:].indirect(l1[:, ent]), prods[t][:, c, :], ALU.subtract)
-            dst = z_bf[:, :, 64 * c : 64 * (c + 1), :].rearrange("p u m t -> p m u t")
-            src = z[:].rearrange("p t (m u) -> p m u t", u=PACK)
-            if c == 0:
-                nc.scalar.copy(dst, src)
-            else:
-                nc.vector.quantize_mx(z2_w[:].bitcast(FP8X4), z2_s[:], z2_bf[:].rearrange("p v t -> p (v t)"))
+                nc.vector.tensor_tensor(z[:, t, :], y_win[t][:].indirect(l1[:, lo // 16 : hi // 16]), prods[:, t, lo:hi], ALU.subtract)
+            dst = z_bf[:, :, lo // PACK : hi // PACK, :].rearrange("p u m t -> p m u t")
+            src = z.rearrange("p t (m u) -> p m u t", u=PACK)
+            if last:
+                quantise_z2(0, HALF)
                 nc.vector.tensor_copy(dst, src)
+                quantise_z2(HALF, S)
+            else:
+                nc.scalar.copy(dst, src)
 
         z_w = keep.tile([P, PACK, P], U32, name="z_w", align_bytes=64)
         z_s = keep.tile([P, PACK, P], U8, name="z_s", align_bytes=64)
         s_win, s_plain = [], []
         for u in range(PACK):
             nc.vector.quantize_mx(z_w[:, u, :].bitcast(FP8X4), z_s[:, u, :], z_bf[:, u].rearrange("p m t -> p (m t)"))
-            acc = psum.tile([P, S], F32, name="acc")
-            nc.tensor.matmul_mx(
-                acc[:], lhsT=z_w[:, u, :].bitcast(FP8X4), lhsT_scale=z_s[:, u, :],
-                rhs=z2_w[:].bitcast(FP8X4), rhs_scale=z2_s[:], start=True, stop=True,
-            )
             win = keep.tile([P, 2 * S], F32, name="s%d" % u)
             plain = keep.tile([P, S], F32, name="sp%d" % u)
-            nc.scalar.activation(win[:, 0:S], acc[:], ACT.Copy, scale=0.0625)
-            nc.scalar.activation(plain[:], acc[:], ACT.Copy, scale=0.0625)
+            spans = ((0, HALF), (HALF, S)) if u == 0 else ((0, S),)
+            accs = []
+            for lo, hi in spans:
+                acc = psum.tile([P, S], F32, name="acc")
+                nc.tensor.matmul_mx(
+                    acc[:, 0 : hi - lo], lhsT=z_w[:, u, :].bitcast(FP8X4), lhsT_scale=z_s[:, u, :],
+                    rhs=z2_w[:, lo:hi].bitcast(FP8X4), rhs_scale=z2_s[:, lo:hi], start=True, stop=True,
+                )
+                accs.append(acc[:, 0 : hi - lo])
+            if u > 0:
+                nc.scalar.activation(win[:, 0:S], accs[0], ACT.Copy, scale=0.0625)
+                nc.scalar.activation(plain[:], accs[0], ACT.Copy, scale=0.0625)
+            else:
+                nc.scalar.activation(win[:, 0:HALF], accs[0], ACT.Copy, scale=0.0625)
+                nc.vector.tensor_scalar(win[:, HALF:S], accs[1], 0.0625, None, ALU.mult)
+                nc.scalar.activation(plain[:, HALF:S], accs[1], ACT.Copy, scale=0.0625)
+                nc.vector.tensor_scalar(plain[:, 0:HALF], accs[0], 0.0625, None, ALU.mult)
             s_win.append(win)
             s_plain.append(plain)
 
-        o_bf = keep.tile([P, S, PACK], BF16, name="o_bf", align_bytes=64)
         o_w = keep.tile([P, S], U32, name="o_w", align_bytes=64)
         o_s = keep.tile([P, S], U8, name="o_s", align_bytes=64)
         out_rows = out_0.rearrange("(p u) v -> p u v", u=PACK)
         out_words = out_1[0].rearrange("p n t -> p (n t)").bitcast(I32)
         first = keep.tile([P, PACK, S], F32, name="first")
         second = keep.tile([P, PACK, S], F32, name="second")
-        larger = keep.tile([P, PACK, S], F32, name="larger")
-        for u in range(PACK + 1):
-            if u < PACK:
-                nc.vector.tensor_tensor(first[:, u, :], s_win[u][:].indirect(l6[:]), s_plain[u][:], ALU.subtract)
+        larger = []
+
+        def larger_of(u):
+            top = keep.tile([P, S], F32, name="s%d" % (u + 1))
+            nc.vector.tensor_tensor(top[:], first[:, u, :], second[:, u, :], ALU.max)
+            larger.append(top)
+
+        for u in range(PACK):
+            nc.vector.tensor_tensor(first[:, u, :], s_win[u][:].indirect(l6[:]), s_plain[u][:], ALU.subtract)
+            nc.vector.tensor_tensor(second[:, u, :], s_win[u][:].indirect(l7[:]), s_plain[u][:], ALU.subtract)
             if u > 0:
-                nc.vector.tensor_tensor(larger[:, u - 1, :], first[:, u - 1, :], second[:, u - 1, :], ALU.max)
-            if u < PACK:
-                nc.vector.tensor_tensor(second[:, u, :], s_win[u][:].indirect(l7[:]), s_plain[u][:], ALU.subtract)
-        for c in range(2):
-            cols = slice(HALF * c, HALF * (c + 1))
-            ent = slice(16 * c, 16 * (c + 1))
-            o = keep.tile([P, PACK, HALF], F32, name="o%d" % c)
+                larger_of(u - 1)
+        larger_of(PACK - 1)
+
+        o_bf = []
+
+        def hand_on(c):
+            lo, hi = CHUNKS[c]
+            nc.vector.quantize_mx(o_w[:, lo:hi].bitcast(FP8X4), o_s[:, lo:hi], o_bf[c][:].rearrange("p v u -> p (v u)"))
+
+        o_all = keep.tile([P, PACK * S], F32, name="second")
+        for c, (lo, hi) in enumerate(CHUNKS):
+            o = o_all[:, PACK * lo : PACK * hi].rearrange("p (u v) -> p u v", u=PACK)
             for u in range(PACK):
-                nc.vector.tensor_tensor(o[:, u, :], s_win[u][:].indirect(l5[:, ent]), larger[:, u, cols], ALU.subtract)
-                if u % 2 == 1:
-                    nc.sync.dma_start(out_rows[:, u - 1 : u + 1, cols], o[:, u - 1 : u + 1, :])
-            src = o[:].rearrange("p u v -> p v u")
-            if c == 0:
-                nc.scalar.copy(o_bf[:, cols, :], src)
+                nc.vector.tensor_tensor(o[:, u, :], s_plain[u][:].indirect(l5[:, lo // 16 : hi // 16]), larger[u][:, lo:hi], ALU.subtract)
+            nc.sync.dma_start(out_rows[:, :, lo:hi], o)
+            if hi == S:
+                hand_on(0)
+            rounded = keep.tile([P, hi - lo, PACK], BF16, name="o_bf%d" % (c % 2), align_bytes=64)
+            o_bf.append(rounded)
+            if hi == S:
+                nc.vector.tensor_copy(rounded[:], o.rearrange("p u v -> p v u"))
             else:
-                nc.vector.tensor_copy(o_bf[:, cols, :], src)
-            nc.vector.quantize_mx(o_w[:, cols].bitcast(FP8X4), o_s[:, cols], o_bf[:, cols, :].rearrange("p v u -> p (v u)"))
-            nc.sync.dma_start(out_words[:, cols], o_w[:, cols].bitcast(I32))
+                nc.scalar.copy(rounded[:], o.rearrange("p u v -> p v u"))
+        hand_on(1)
+        lo, hi = CHUNKS[-1]
+        nc.sync.dma_start(out_words[:, 0:lo], o_w[:, 0:lo].bitcast(I32))
+        hand_on(2)
+        nc.scalar.dma_start(out_words[:, lo:hi], o_w[:, lo:hi].bitcast(I32))
         for q in range(4):
             queue = nc.scalar if q % 2 else nc.sync
             queue.dma_start(out_2[0, 4 * q : 4 * q + 4, :].bitcast(I32), o_s[32 * q : 32 * q + 4, :].bitcast(I32))

@@ -3,7 +3,9 @@ from contextlib import ExitStack
 import concourse.mybir as mybir
 from concourse.masks import make_identity
 
-K, T, S, W = 512, 2048, 512, 256
+T = 2048
+S = 512
+W = 256
 FLOPS = 4 * 2 * 512 * 512 * 512
 
 F32 = mybir.dt.float32
@@ -19,7 +21,13 @@ ACT = mybir.ActivationFunctionType
 
 P = 128
 PACK = 4
-HALF = 256
+QUADRANTS = 4
+BLOCKS = 16
+RUN = 8
+LANES = 16
+BANKS = 8
+HALF = S // 2
+S_SCALE = 0.0625
 CHUNKS = ((0, 256), (256, 384), (384, 512))
 
 
@@ -30,39 +38,42 @@ def tile_picked_twksoftbdueltrim_none_po_kernel(
     nc = tc.nc
     with ExitStack() as ctx:
         keep = ctx.enter_context(tc.tile_pool(name="keep", bufs=1))
-        psum = ctx.enter_context(tc.psum_pool(name="psum", bufs=8))
+        psum = ctx.enter_context(tc.psum_pool(name="psum", bufs=BANKS))
 
         def load_list(name, src):
-            t = keep.tile(list(src.shape), U16, name=name)
-            nc.sync.dma_start(t[:], src)
-            return t
+            offsets = keep.tile(list(src.shape), U16, name=name)
+            nc.sync.dma_start(offsets[:], src)
+            return offsets
 
-        def load_scale_rows(tile, src, eng):
-            eng.memset(tile[:].bitcast(I32), 0)
-            for q in range(4):
-                nc.sync.dma_start(tile[32 * q : 32 * q + 4, :].bitcast(I32), src[0, 4 * q : 4 * q + 4, :].bitcast(I32))
+        def entries(offsets, lo, hi):
+            return offsets[:, lo // LANES : hi // LANES]
+
+        def load_scale_rows(plane, src):
+            nc.gpsimd.memset(plane[:].bitcast(I32), 0)
+            for q in range(QUADRANTS):
+                nc.sync.dma_start(plane[32 * q : 32 * q + 4, :].bitcast(I32), src[0, 4 * q : 4 * q + 4, :].bitcast(I32))
 
         def load_weight(name, words, scales):
-            raw_w = keep.tile([P, 2 * S], U8, name=name + "_raw_words")
-            raw_s = keep.tile([P, S], U8, name=name + "_raw_scales")
-            nc.sync.dma_start(raw_w[:].bitcast(I32), words[0].bitcast(I32))
-            load_scale_rows(raw_s, scales, nc.gpsimd)
-            return raw_w, raw_s
+            raw_words = keep.tile([P, 2 * S], U8, name=name + "_raw_words")
+            raw_scales = keep.tile([P, S], U8, name=name + "_raw_scales")
+            nc.sync.dma_start(raw_words[:].bitcast(I32), words[0].bitcast(I32))
+            load_scale_rows(raw_scales, scales)
+            return raw_words, raw_scales
 
         def deal_weight(name, raw):
-            dealt_w = keep.tile([P, 2 * S], U8, name=name + "_words", align_bytes=64)
-            dealt_s = keep.tile([P, S], U8, name=name + "_scales", align_bytes=64)
-            for dst, src in ((dealt_w, raw[0]), (dealt_s, raw[1])):
+            words = keep.tile([P, 2 * S], U8, name=name + "_words", align_bytes=64)
+            scales = keep.tile([P, S], U8, name=name + "_scales", align_bytes=64)
+            for dst, src in zip((words, scales), raw):
                 nc.gpsimd.tensor_copy(
-                    dst[:].bitcast(I32).rearrange("p (t b r) -> p t b r", t=PACK, b=16),
-                    src[:].bitcast(I32).rearrange("p (b t r) -> p t b r", t=PACK, b=16),
+                    dst[:].bitcast(I32).rearrange("p (t b r) -> p t b r", t=PACK, b=BLOCKS),
+                    src[:].bitcast(I32).rearrange("p (b t r) -> p t b r", t=PACK, b=BLOCKS),
                 )
-            return dealt_w, dealt_s
+            return words, scales
 
-        def pick(name, dtype, table, lst):
-            t = keep.tile([P, S], dtype, name=name, align_bytes=64)
-            nc.vector.tensor_copy(t[:], table[:].indirect(lst[:]))
-            return t
+        def pick(name, dtype, table, offsets):
+            picked = keep.tile([P, S], dtype, name=name, align_bytes=64)
+            nc.vector.tensor_copy(picked[:], table[:].indirect(offsets[:]))
+            return picked
 
         def project(weight, words, scales, t):
             acc = psum.tile([P, S], F32, name="acc")
@@ -79,7 +90,7 @@ def tile_picked_twksoftbdueltrim_none_po_kernel(
 
         xs = keep.tile([P, T], U8, name="xs")
         xw = keep.tile([P, T], U32, name="xw")
-        load_scale_rows(xs, x_scales, nc.gpsimd)
+        load_scale_rows(xs, x_scales)
         l_three = load_list("three", three)
         l_two = load_list("two", two)
         nc.sync.dma_start(xw[:].bitcast(I32), x_words[0].rearrange("p n t -> p (n t)").bitcast(I32))
@@ -91,10 +102,10 @@ def tile_picked_twksoftbdueltrim_none_po_kernel(
         ident = keep.tile([P, P], F32, name="ident")
         nc.gpsimd.memset(gain_rows[:], 0.0)
         make_identity(nc, ident[:])
-        for i, g in enumerate((ga, gb)):
+        for i, gain in enumerate((ga, gb)):
             nc.sync.dma_start(
-                gain_rows[PACK * i : PACK * (i + 1), :].rearrange("t (b r) -> t b r", r=8),
-                g.rearrange("(b t r) o -> t b (r o)", t=PACK, r=8),
+                gain_rows[PACK * i : PACK * (i + 1), :].rearrange("t (b r) -> t b r", r=RUN),
+                gain.rearrange("(b t r) o -> t b (r o)", t=PACK, r=RUN),
             )
         raw2 = load_weight("w2", w2_words, w2_scales)
         raw1 = load_weight("w1", w1_words, w1_scales)
@@ -104,22 +115,22 @@ def tile_picked_twksoftbdueltrim_none_po_kernel(
         l7 = load_list("n7", n7)
         l5 = load_list("n5", n5)
 
-        s_three = pick("s_three", U8, xs, l_three)
-        s_two = pick("s_two", U8, xs, l_two)
-        w_three = pick("w_three", U32, xw, l_three)
+        scales_three = pick("scales_three", U8, xs, l_three)
+        scales_two = pick("scales_two", U8, xs, l_two)
+        words_three = pick("words_three", U32, xw, l_three)
         w3 = deal_weight("w3", raw3)
-        s_offs = pick("s_offs", U8, xs, l_offs)
-        w_two = pick("w_two", U32, xw, l_two)
-        w_offs = pick("w_offs", U32, xw, l_offs)
+        scales_offs = pick("scales_offs", U8, xs, l_offs)
+        words_two = pick("words_two", U32, xw, l_two)
+        words_offs = pick("words_offs", U32, xw, l_offs)
 
-        gain_t = psum.tile([P, S], F32, name="acc")
-        nc.tensor.transpose(gain_t[:, 0:P], gain_rows[:], ident[:])
+        gains_turned = psum.tile([P, S], F32, name="acc")
+        nc.tensor.transpose(gains_turned[:, 0:P], gain_rows[:], ident[:])
         gains = keep.tile([P, 2 * PACK], F32, name="gains")
-        nc.scalar.copy(gains[:], gain_t[:, 0 : 2 * PACK])
+        nc.scalar.copy(gains[:], gains_turned[:, 0 : 2 * PACK])
 
         b_win = []
         for t in range(PACK):
-            acc = project(w3, w_three, s_three, t)
+            acc = project(w3, words_three, scales_three, t)
             win = keep.tile([P, S], F32, name="b%d" % t)
             nc.scalar.copy(win[:], acc[:])
             b_win.append(win)
@@ -135,9 +146,9 @@ def tile_picked_twksoftbdueltrim_none_po_kernel(
             for side in range(2):
                 nc.vector.tensor_copy(pairs[t // 2][:, side, t % 2, :], b_win[t][:].indirect(pair_lists[side][:]))
 
-        def duel(h):
-            diff = keep.tile([P, 2, W], F32, name="b%d" % (2 - 2 * h))
-            nc.vector.tensor_tensor(diff[:], pairs[h][:, 0], pairs[h][:, 1], ALU.subtract)
+        def duel(h, engine):
+            diff = keep.tile([P, 2, W], F32, name="diff%d" % h)
+            engine.tensor_tensor(diff[:], pairs[h][:, 0], pairs[h][:, 1], ALU.subtract)
             nc.scalar.activation(gates[h][:, 0], diff[:], ACT.Sigmoid)
             nc.scalar.activation(gates[h][:, 1], diff[:], ACT.Sigmoid, scale=-1.0)
 
@@ -150,22 +161,21 @@ def tile_picked_twksoftbdueltrim_none_po_kernel(
                     if side == 1:
                         nc.scalar.activation(z2_rows[:, t, :], dts[t][:], ACT.Copy, scale=gains[:, PACK + t : PACK + t + 1])
 
-        for t in range(PACK - 1):
-            fetch(t)
-        duel(0)
-        fetch(PACK - 1)
-        duel(1)
+        for h, engine in enumerate((nc.gpsimd, nc.vector)):
+            fetch(2 * h)
+            fetch(2 * h + 1)
+            duel(h, engine)
 
         d_win, y_win, tanh_d = [], [], []
         for t in range(PACK):
-            acc = project(w2, w_two, s_two, t)
+            acc = project(w2, words_two, scales_two, t)
             win = keep.tile([P, 2 * S], F32, name="d%d" % t)
-            th = keep.tile([P, S], F32, name="tanh%d" % t)
+            tanh = keep.tile([P, S], F32, name="tanh%d" % t)
             nc.scalar.activation(win[:, 0:S], acc[:], ACT.Copy, scale=gains[:, t : t + 1])
-            nc.scalar.activation(th[:], acc[:], ACT.Tanh)
+            nc.scalar.activation(tanh[:], acc[:], ACT.Tanh)
             d_win.append(win)
-            tanh_d.append(th)
-            acc = project(w1, w_offs, s_offs, t)
+            tanh_d.append(tanh)
+            acc = project(w1, words_offs, scales_offs, t)
             win = keep.tile([P, S], F32, name="y%d" % t)
             nc.scalar.activation(win[:], acc[:], ACT.Copy, scale=gains[:, t : t + 1])
             y_win.append(win)
@@ -174,69 +184,70 @@ def tile_picked_twksoftbdueltrim_none_po_kernel(
         put(1)
         z2_bf = keep.tile([P, S, PACK], BF16, name="z2_bf", align_bytes=64)
         nc.scalar.copy(z2_bf[:], z2_rows[:].rearrange("p t v -> p v t"))
-        z2_w = keep.tile([P, S], U32, name="z2_w", align_bytes=64)
-        z2_s = keep.tile([P, S], U8, name="z2_s", align_bytes=64)
-        prods = keep.tile([P, PACK, S], F32, name="pairs1")
+        z2_words = keep.tile([P, S], U32, name="z2_words", align_bytes=64)
+        z2_scales = keep.tile([P, S], U8, name="z2_scales", align_bytes=64)
+
+        prods = keep.tile([P, PACK, S], F32, name="prods", tag="pairs1")
         for t in range(PACK):
             nc.vector.tensor_tensor(prods[:, t, :], d_win[t][:].indirect(l2[:]), tanh_d[t][:], ALU.mult)
 
         z_bf = keep.tile([P, PACK, P, PACK], BF16, name="z_bf", align_bytes=64)
 
         def quantise_z2(lo, hi):
-            nc.vector.quantize_mx(z2_w[:, lo:hi].bitcast(FP8X4), z2_s[:, lo:hi], z2_bf[:, lo:hi, :].rearrange("p v t -> p (v t)"))
+            nc.vector.quantize_mx(
+                z2_words[:, lo:hi].bitcast(FP8X4), z2_scales[:, lo:hi], z2_bf[:, lo:hi, :].rearrange("p v t -> p (v t)")
+            )
 
-        z_all = keep.tile([P, PACK * S], F32, name="z2_rows")
+        z_all = keep.tile([P, PACK * S], F32, name="z", tag="z2_rows")
         for lo, hi in CHUNKS:
-            last = hi == S
             z = z_all[:, PACK * lo : PACK * hi].rearrange("p (t j) -> p t j", t=PACK)
             for t in range(PACK):
-                nc.vector.tensor_tensor(z[:, t, :], y_win[t][:].indirect(l1[:, lo // 16 : hi // 16]), prods[:, t, lo:hi], ALU.subtract)
+                nc.vector.tensor_tensor(z[:, t, :], y_win[t][:].indirect(entries(l1, lo, hi)), prods[:, t, lo:hi], ALU.subtract)
             dst = z_bf[:, :, lo // PACK : hi // PACK, :].rearrange("p u m t -> p m u t")
             src = z.rearrange("p t (m u) -> p m u t", u=PACK)
-            if last:
+            if hi == S:
                 quantise_z2(0, HALF)
                 nc.vector.tensor_copy(dst, src)
                 quantise_z2(HALF, S)
             else:
                 nc.scalar.copy(dst, src)
 
-        z_w = keep.tile([P, PACK, P], U32, name="z_w", align_bytes=64)
-        z_s = keep.tile([P, PACK, P], U8, name="z_s", align_bytes=64)
+        z_words = keep.tile([P, PACK, P], U32, name="z_words", align_bytes=64)
+        z_scales = keep.tile([P, PACK, P], U8, name="z_scales", align_bytes=64)
         s_win, s_plain = [], []
         for u in range(PACK):
-            nc.vector.quantize_mx(z_w[:, u, :].bitcast(FP8X4), z_s[:, u, :], z_bf[:, u].rearrange("p m t -> p (m t)"))
+            nc.vector.quantize_mx(z_words[:, u, :].bitcast(FP8X4), z_scales[:, u, :], z_bf[:, u].rearrange("p m t -> p (m t)"))
             win = keep.tile([P, 2 * S], F32, name="s%d" % u)
-            plain = keep.tile([P, S], F32, name="sp%d" % u)
-            spans = ((0, HALF), (HALF, S)) if u == 0 else ((0, S),)
+            plain = keep.tile([P, S], F32, name="s_plain%d" % u)
             accs = []
-            for lo, hi in spans:
+            for lo, hi in ((0, HALF), (HALF, S)) if u == 0 else ((0, S),):
                 acc = psum.tile([P, S], F32, name="acc")
                 nc.tensor.matmul_mx(
-                    acc[:, 0 : hi - lo], lhsT=z_w[:, u, :].bitcast(FP8X4), lhsT_scale=z_s[:, u, :],
-                    rhs=z2_w[:, lo:hi].bitcast(FP8X4), rhs_scale=z2_s[:, lo:hi], start=True, stop=True,
+                    acc[:, 0 : hi - lo], lhsT=z_words[:, u, :].bitcast(FP8X4), lhsT_scale=z_scales[:, u, :],
+                    rhs=z2_words[:, lo:hi].bitcast(FP8X4), rhs_scale=z2_scales[:, lo:hi], start=True, stop=True,
                 )
                 accs.append(acc[:, 0 : hi - lo])
-            if u > 0:
-                nc.scalar.activation(win[:, 0:S], accs[0], ACT.Copy, scale=0.0625)
-                nc.scalar.activation(plain[:], accs[0], ACT.Copy, scale=0.0625)
+            if u == 0:
+                nc.scalar.activation(win[:, 0:HALF], accs[0], ACT.Copy, scale=S_SCALE)
+                nc.vector.tensor_scalar(win[:, HALF:S], accs[1], S_SCALE, None, ALU.mult)
+                nc.scalar.activation(plain[:, HALF:S], accs[1], ACT.Copy, scale=S_SCALE)
+                nc.vector.tensor_scalar(plain[:, 0:HALF], accs[0], S_SCALE, None, ALU.mult)
             else:
-                nc.scalar.activation(win[:, 0:HALF], accs[0], ACT.Copy, scale=0.0625)
-                nc.vector.tensor_scalar(win[:, HALF:S], accs[1], 0.0625, None, ALU.mult)
-                nc.scalar.activation(plain[:, HALF:S], accs[1], ACT.Copy, scale=0.0625)
-                nc.vector.tensor_scalar(plain[:, 0:HALF], accs[0], 0.0625, None, ALU.mult)
+                nc.scalar.activation(win[:, 0:S], accs[0], ACT.Copy, scale=S_SCALE)
+                nc.scalar.activation(plain[:], accs[0], ACT.Copy, scale=S_SCALE)
             s_win.append(win)
             s_plain.append(plain)
 
-        o_w = keep.tile([P, S], U32, name="o_w", align_bytes=64)
-        o_s = keep.tile([P, S], U8, name="o_s", align_bytes=64)
+        out_words = keep.tile([P, S], U32, name="out_words", align_bytes=64)
+        out_scales = keep.tile([P, S], U8, name="out_scales", align_bytes=64)
         out_rows = out_0.rearrange("(p u) v -> p u v", u=PACK)
-        out_words = out_1[0].rearrange("p n t -> p (n t)").bitcast(I32)
+        out_codes = out_1[0].rearrange("p n t -> p (n t)").bitcast(I32)
         first = keep.tile([P, PACK, S], F32, name="first")
         second = keep.tile([P, PACK, S], F32, name="second")
         larger = []
 
         def larger_of(u):
-            top = keep.tile([P, S], F32, name="s%d" % (u + 1))
+            top = keep.tile([P, S], F32, name="larger%d" % u, tag="s%d" % (u + 1))
             nc.vector.tensor_tensor(top[:], first[:, u, :], second[:, u, :], ALU.max)
             larger.append(top)
 
@@ -247,31 +258,33 @@ def tile_picked_twksoftbdueltrim_none_po_kernel(
                 larger_of(u - 1)
         larger_of(PACK - 1)
 
-        o_bf = []
+        out_bf = []
 
-        def hand_on(c):
+        def quantise_out(c):
             lo, hi = CHUNKS[c]
-            nc.vector.quantize_mx(o_w[:, lo:hi].bitcast(FP8X4), o_s[:, lo:hi], o_bf[c][:].rearrange("p v u -> p (v u)"))
+            nc.vector.quantize_mx(
+                out_words[:, lo:hi].bitcast(FP8X4), out_scales[:, lo:hi], out_bf[c][:].rearrange("p v u -> p (v u)")
+            )
 
-        o_all = keep.tile([P, PACK * S], F32, name="second")
+        result = keep.tile([P, PACK * S], F32, name="result", tag="second")
         for c, (lo, hi) in enumerate(CHUNKS):
-            o = o_all[:, PACK * lo : PACK * hi].rearrange("p (u v) -> p u v", u=PACK)
+            o = result[:, PACK * lo : PACK * hi].rearrange("p (u v) -> p u v", u=PACK)
             for u in range(PACK):
-                nc.vector.tensor_tensor(o[:, u, :], s_plain[u][:].indirect(l5[:, lo // 16 : hi // 16]), larger[u][:, lo:hi], ALU.subtract)
+                nc.vector.tensor_tensor(o[:, u, :], s_plain[u][:].indirect(entries(l5, lo, hi)), larger[u][:, lo:hi], ALU.subtract)
             nc.sync.dma_start(out_rows[:, :, lo:hi], o)
             if hi == S:
-                hand_on(0)
-            rounded = keep.tile([P, hi - lo, PACK], BF16, name="o_bf%d" % (c % 2), align_bytes=64)
-            o_bf.append(rounded)
+                quantise_out(0)
+            rounded = keep.tile([P, hi - lo, PACK], BF16, name="out_bf%d" % (c % 2), align_bytes=64)
+            out_bf.append(rounded)
             if hi == S:
                 nc.vector.tensor_copy(rounded[:], o.rearrange("p u v -> p v u"))
             else:
                 nc.scalar.copy(rounded[:], o.rearrange("p u v -> p v u"))
-        hand_on(1)
-        lo, hi = CHUNKS[-1]
-        nc.sync.dma_start(out_words[:, 0:lo], o_w[:, 0:lo].bitcast(I32))
-        hand_on(2)
-        nc.scalar.dma_start(out_words[:, lo:hi], o_w[:, lo:hi].bitcast(I32))
-        for q in range(4):
+        last_lo = CHUNKS[2][0]
+        quantise_out(1)
+        nc.sync.dma_start(out_codes[:, 0:last_lo], out_words[:, 0:last_lo].bitcast(I32))
+        quantise_out(2)
+        nc.scalar.dma_start(out_codes[:, last_lo:S], out_words[:, last_lo:S].bitcast(I32))
+        for q in range(QUADRANTS):
             queue = nc.scalar if q % 2 else nc.sync
-            queue.dma_start(out_2[0, 4 * q : 4 * q + 4, :].bitcast(I32), o_s[32 * q : 32 * q + 4, :].bitcast(I32))
+            queue.dma_start(out_2[0, 4 * q : 4 * q + 4, :].bitcast(I32), out_scales[32 * q : 32 * q + 4, :].bitcast(I32))

from contextlib import ExitStack

import concourse.mybir as mybir
from concourse.masks import make_identity

T = 2048
S = 512
W = 256
FLOPS = 4 * 2 * 512 * 512 * 512

F32 = mybir.dt.float32
BF16 = mybir.dt.bfloat16
I32 = mybir.dt.int32
U32 = mybir.dt.uint32
U16 = mybir.dt.uint16
U8 = mybir.dt.uint8
FP8X4 = mybir.dt.float8_e4m3fn_x4
FP4X4 = mybir.dt.float4_e2m1fn_x4
ALU = mybir.AluOpType
ACT = mybir.ActivationFunctionType

P = 128
PACK = 4
QUADRANTS = 4
BLOCKS = 16
RUN = 8
LANES = 16
BANKS = 8
HALF = S // 2
S_SCALE = 0.0625
CHUNKS = ((0, 256), (256, 384), (384, 512))


def tile_picked_twksoftbdueltrim_none_po_kernel(
    tc, x_words, x_scales, w1_words, w1_scales, w2_words, w2_scales, w3_words, w3_scales,
    ga, gb, offs, two, n1, n2, three, n3, n4, n5, n6, n7, out_0, out_1, out_2,
):
    nc = tc.nc
    with ExitStack() as ctx:
        keep = ctx.enter_context(tc.tile_pool(name="keep", bufs=1))
        psum = ctx.enter_context(tc.psum_pool(name="psum", bufs=BANKS))

        def load_list(name, src):
            offsets = keep.tile(list(src.shape), U16, name=name)
            nc.sync.dma_start(offsets[:], src)
            return offsets

        def entries(offsets, lo, hi):
            return offsets[:, lo // LANES : hi // LANES]

        def load_scale_rows(plane, src):
            nc.gpsimd.memset(plane[:].bitcast(I32), 0)
            for q in range(QUADRANTS):
                nc.sync.dma_start(plane[32 * q : 32 * q + 4, :].bitcast(I32), src[0, 4 * q : 4 * q + 4, :].bitcast(I32))

        def load_weight(name, words, scales):
            raw_words = keep.tile([P, 2 * S], U8, name=name + "_raw_words")
            raw_scales = keep.tile([P, S], U8, name=name + "_raw_scales")
            nc.sync.dma_start(raw_words[:].bitcast(I32), words[0].bitcast(I32))
            load_scale_rows(raw_scales, scales)
            return raw_words, raw_scales

        def deal_weight(name, raw):
            words = keep.tile([P, 2 * S], U8, name=name + "_words", align_bytes=64)
            scales = keep.tile([P, S], U8, name=name + "_scales", align_bytes=64)
            for dst, src in zip((words, scales), raw):
                nc.gpsimd.tensor_copy(
                    dst[:].bitcast(I32).rearrange("p (t b r) -> p t b r", t=PACK, b=BLOCKS),
                    src[:].bitcast(I32).rearrange("p (b t r) -> p t b r", t=PACK, b=BLOCKS),
                )
            return words, scales

        def pick(name, dtype, table, offsets):
            picked = keep.tile([P, S], dtype, name=name, align_bytes=64)
            nc.vector.tensor_copy(picked[:], table[:].indirect(offsets[:]))
            return picked

        def project(weight, words, scales, t):
            acc = psum.tile([P, S], F32, name="acc")
            nc.tensor.matmul_mx(
                acc[:],
                lhsT=weight[0][:, 2 * P * t : 2 * P * (t + 1)].bitcast(FP4X4),
                lhsT_scale=weight[1][:, P * t : P * (t + 1)],
                rhs=words[:].bitcast(FP8X4),
                rhs_scale=scales[:],
                start=True,
                stop=True,
            )
            return acc

        xs = keep.tile([P, T], U8, name="xs")
        xw = keep.tile([P, T], U32, name="xw")
        load_scale_rows(xs, x_scales)
        l_three = load_list("three", three)
        l_two = load_list("two", two)
        nc.sync.dma_start(xw[:].bitcast(I32), x_words[0].rearrange("p n t -> p (n t)").bitcast(I32))
        l_offs = load_list("offs", offs)
        raw3 = load_weight("w3", w3_words, w3_scales)
        l3 = load_list("n3", n3)
        l4 = load_list("n4", n4)
        gain_rows = keep.tile([P, P], F32, name="gain_rows")
        ident = keep.tile([P, P], F32, name="ident")
        nc.gpsimd.memset(gain_rows[:], 0.0)
        make_identity(nc, ident[:])
        for i, gain in enumerate((ga, gb)):
            nc.sync.dma_start(
                gain_rows[PACK * i : PACK * (i + 1), :].rearrange("t (b r) -> t b r", r=RUN),
                gain.rearrange("(b t r) o -> t b (r o)", t=PACK, r=RUN),
            )
        raw2 = load_weight("w2", w2_words, w2_scales)
        raw1 = load_weight("w1", w1_words, w1_scales)
        l2 = load_list("n2", n2)
        l1 = load_list("n1", n1)
        l6 = load_list("n6", n6)
        l7 = load_list("n7", n7)
        l5 = load_list("n5", n5)

        scales_three = pick("scales_three", U8, xs, l_three)
        scales_two = pick("scales_two", U8, xs, l_two)
        words_three = pick("words_three", U32, xw, l_three)
        w3 = deal_weight("w3", raw3)
        scales_offs = pick("scales_offs", U8, xs, l_offs)
        words_two = pick("words_two", U32, xw, l_two)
        words_offs = pick("words_offs", U32, xw, l_offs)

        gains_turned = psum.tile([P, S], F32, name="acc")
        nc.tensor.transpose(gains_turned[:, 0:P], gain_rows[:], ident[:])
        gains = keep.tile([P, 2 * PACK], F32, name="gains")
        nc.scalar.copy(gains[:], gains_turned[:, 0 : 2 * PACK])

        b_win = []
        for t in range(PACK):
            acc = project(w3, words_three, scales_three, t)
            win = keep.tile([P, S], F32, name="b%d" % t)
            nc.scalar.copy(win[:], acc[:])
            b_win.append(win)
        w2 = deal_weight("w2", raw2)
        w1 = deal_weight("w1", raw1)
        pairs = [keep.tile([P, 2, 2, W], F32, name="pairs%d" % h) for h in range(2)]
        gates = [keep.tile([P, 2, 2, W], F32, name="gates%d" % h) for h in range(2)]
        dts = [keep.tile([P, S], F32, name="dt%d" % t) for t in range(PACK)]
        z2_rows = keep.tile([P, PACK, S], BF16, name="z2_rows")
        pair_lists = (l3, l4)

        def fetch(t):
            for side in range(2):
                nc.vector.tensor_copy(pairs[t // 2][:, side, t % 2, :], b_win[t][:].indirect(pair_lists[side][:]))

        def duel(h, engine):
            diff = keep.tile([P, 2, W], F32, name="diff%d" % h)
            engine.tensor_tensor(diff[:], pairs[h][:, 0], pairs[h][:, 1], ALU.subtract)
            nc.scalar.activation(gates[h][:, 0], diff[:], ACT.Sigmoid)
            nc.scalar.activation(gates[h][:, 1], diff[:], ACT.Sigmoid, scale=-1.0)

        def put(h):
            for side in range(2):
                for t in (2 * h, 2 * h + 1):
                    nc.vector.tensor_tensor(
                        dts[t][:].indirect(pair_lists[side][:]), pairs[h][:, side, t % 2, :], gates[h][:, side, t % 2, :], ALU.mult
                    )
                    if side == 1:
                        nc.scalar.activation(z2_rows[:, t, :], dts[t][:], ACT.Copy, scale=gains[:, PACK + t : PACK + t + 1])

        for h, engine in enumerate((nc.gpsimd, nc.vector)):
            fetch(2 * h)
            fetch(2 * h + 1)
            duel(h, engine)

        d_win, y_win, tanh_d = [], [], []
        for t in range(PACK):
            acc = project(w2, words_two, scales_two, t)
            win = keep.tile([P, 2 * S], F32, name="d%d" % t)
            tanh = keep.tile([P, S], F32, name="tanh%d" % t)
            nc.scalar.activation(win[:, 0:S], acc[:], ACT.Copy, scale=gains[:, t : t + 1])
            nc.scalar.activation(tanh[:], acc[:], ACT.Tanh)
            d_win.append(win)
            tanh_d.append(tanh)
            acc = project(w1, words_offs, scales_offs, t)
            win = keep.tile([P, S], F32, name="y%d" % t)
            nc.scalar.activation(win[:], acc[:], ACT.Copy, scale=gains[:, t : t + 1])
            y_win.append(win)

        put(0)
        put(1)
        z2_bf = keep.tile([P, S, PACK], BF16, name="z2_bf", align_bytes=64)
        nc.scalar.copy(z2_bf[:], z2_rows[:].rearrange("p t v -> p v t"))
        z2_words = keep.tile([P, S], U32, name="z2_words", align_bytes=64)
        z2_scales = keep.tile([P, S], U8, name="z2_scales", align_bytes=64)

        prods = keep.tile([P, PACK, S], F32, name="prods", tag="pairs1")
        for t in range(PACK):
            nc.vector.tensor_tensor(prods[:, t, :], d_win[t][:].indirect(l2[:]), tanh_d[t][:], ALU.mult)

        z_bf = keep.tile([P, PACK, P, PACK], BF16, name="z_bf", align_bytes=64)

        def quantise_z2(lo, hi):
            nc.vector.quantize_mx(
                z2_words[:, lo:hi].bitcast(FP8X4), z2_scales[:, lo:hi], z2_bf[:, lo:hi, :].rearrange("p v t -> p (v t)")
            )

        z_all = keep.tile([P, PACK * S], F32, name="z", tag="z2_rows")
        for lo, hi in CHUNKS:
            z = z_all[:, PACK * lo : PACK * hi].rearrange("p (t j) -> p t j", t=PACK)
            for t in range(PACK):
                nc.vector.tensor_tensor(z[:, t, :], y_win[t][:].indirect(entries(l1, lo, hi)), prods[:, t, lo:hi], ALU.subtract)
            dst = z_bf[:, :, lo // PACK : hi // PACK, :].rearrange("p u m t -> p m u t")
            src = z.rearrange("p t (m u) -> p m u t", u=PACK)
            if hi == S:
                quantise_z2(0, HALF)
                nc.vector.tensor_copy(dst, src)
                quantise_z2(HALF, S)
            else:
                nc.scalar.copy(dst, src)

        z_words = keep.tile([P, PACK, P], U32, name="z_words", align_bytes=64)
        z_scales = keep.tile([P, PACK, P], U8, name="z_scales", align_bytes=64)
        s_win, s_plain = [], []
        for u in range(PACK):
            nc.vector.quantize_mx(z_words[:, u, :].bitcast(FP8X4), z_scales[:, u, :], z_bf[:, u].rearrange("p m t -> p (m t)"))
            win = keep.tile([P, 2 * S], F32, name="s%d" % u)
            plain = keep.tile([P, S], F32, name="s_plain%d" % u)
            accs = []
            for lo, hi in ((0, HALF), (HALF, S)) if u == 0 else ((0, S),):
                acc = psum.tile([P, S], F32, name="acc")
                nc.tensor.matmul_mx(
                    acc[:, 0 : hi - lo], lhsT=z_words[:, u, :].bitcast(FP8X4), lhsT_scale=z_scales[:, u, :],
                    rhs=z2_words[:, lo:hi].bitcast(FP8X4), rhs_scale=z2_scales[:, lo:hi], start=True, stop=True,
                )
                accs.append(acc[:, 0 : hi - lo])
            if u == 0:
                nc.scalar.activation(win[:, 0:HALF], accs[0], ACT.Copy, scale=S_SCALE)
                nc.vector.tensor_scalar(win[:, HALF:S], accs[1], S_SCALE, None, ALU.mult)
                nc.scalar.activation(plain[:, HALF:S], accs[1], ACT.Copy, scale=S_SCALE)
                nc.vector.tensor_scalar(plain[:, 0:HALF], accs[0], S_SCALE, None, ALU.mult)
            else:
                nc.scalar.activation(win[:, 0:S], accs[0], ACT.Copy, scale=S_SCALE)
                nc.scalar.activation(plain[:], accs[0], ACT.Copy, scale=S_SCALE)
            s_win.append(win)
            s_plain.append(plain)

        out_words = keep.tile([P, S], U32, name="out_words", align_bytes=64)
        out_scales = keep.tile([P, S], U8, name="out_scales", align_bytes=64)
        out_rows = out_0.rearrange("(p u) v -> p u v", u=PACK)
        out_codes = out_1[0].rearrange("p n t -> p (n t)").bitcast(I32)
        first = keep.tile([P, PACK, S], F32, name="first")
        second = keep.tile([P, PACK, S], F32, name="second")
        larger = []

        def larger_of(u):
            top = keep.tile([P, S], F32, name="larger%d" % u, tag="s%d" % (u + 1))
            nc.vector.tensor_tensor(top[:], first[:, u, :], second[:, u, :], ALU.max)
            larger.append(top)

        for u in range(PACK):
            nc.vector.tensor_tensor(first[:, u, :], s_win[u][:].indirect(l6[:]), s_plain[u][:], ALU.subtract)
            nc.vector.tensor_tensor(second[:, u, :], s_win[u][:].indirect(l7[:]), s_plain[u][:], ALU.subtract)
            if u > 0:
                larger_of(u - 1)
        larger_of(PACK - 1)

        out_bf = []

        def quantise_out(c):
            lo, hi = CHUNKS[c]
            nc.vector.quantize_mx(
                out_words[:, lo:hi].bitcast(FP8X4), out_scales[:, lo:hi], out_bf[c][:].rearrange("p v u -> p (v u)")
            )

        result = keep.tile([P, PACK * S], F32, name="result", tag="second")
        for c, (lo, hi) in enumerate(CHUNKS):
            o = result[:, PACK * lo : PACK * hi].rearrange("p (u v) -> p u v", u=PACK)
            for u in range(PACK):
                nc.vector.tensor_tensor(o[:, u, :], s_plain[u][:].indirect(entries(l5, lo, hi)), larger[u][:, lo:hi], ALU.subtract)
            nc.sync.dma_start(out_rows[:, :, lo:hi], o)
            if hi == S:
                quantise_out(0)
            rounded = keep.tile([P, hi - lo, PACK], BF16, name="out_bf%d" % (c % 2), align_bytes=64)
            out_bf.append(rounded)
            if hi == S:
                nc.vector.tensor_copy(rounded[:], o.rearrange("p u v -> p v u"))
            else:
                nc.scalar.copy(rounded[:], o.rearrange("p u v -> p v u"))
        last_lo = CHUNKS[2][0]
        quantise_out(1)
        nc.sync.dma_start(out_codes[:, 0:last_lo], out_words[:, 0:last_lo].bitcast(I32))
        quantise_out(2)
        nc.scalar.dma_start(out_codes[:, last_lo:S], out_words[:, last_lo:S].bitcast(I32))
        for q in range(QUADRANTS):
            queue = nc.scalar if q % 2 else nc.sync
            queue.dma_start(out_2[0, 4 * q : 4 * q + 4, :].bitcast(I32), out_scales[32 * q : 32 * q + 4, :].bitcast(I32))
